import numpy as np
import ml_dtypes


def mxq(x, axis, fmt="e4m3"):
    dtype, down = {"e4m3": (ml_dtypes.float8_e4m3fn, 7), "e5m2": (ml_dtypes.float8_e5m2, 14)}[fmt]
    v = np.moveaxis(np.asarray(x, np.float32).astype(ml_dtypes.bfloat16).astype(np.float64), axis, -1)
    blocks = v.reshape(v.shape[:-1] + (-1, 32))
    amax = np.abs(blocks).max(-1, keepdims=True)
    byte = np.maximum(np.where(amax > 0, np.frexp(amax)[1] - 1 + 127, 0) - down, 1)
    scale = np.exp2(byte - 127.0)
    codes = (blocks / scale).astype(np.float32).astype(dtype).astype(np.float64)
    return np.moveaxis((codes * scale).reshape(v.shape), -1, axis)


WIDE = False


def mx_kscale(k):
    if not WIDE:
        return np.ones(k)
    levels = np.array([10, -10, 5, -5, 0])
    if k % 512:
        return np.exp2(np.random.permutation(np.resize(levels, k // 32))).repeat(32)
    a = np.empty((k // 512, 16))
    for p in range(k // 512):
        a[p, :8] = np.random.permutation(np.resize(levels, 8))
        for g in range(8):
            far = levels[np.abs(levels - a[p, g]) >= 10]
            a[p, g + 8] = far[np.random.randint(len(far))]
    return np.exp2(a.ravel()).repeat(32)


def f64(x):
    return np.asarray(x).astype(np.float64)


def striped(idx):
    return np.tile(idx.reshape(-1, 16).T, (8, 1)).astype(np.uint16)


def unstriped(offs):
    return offs[:16].T.reshape(-1).astype(np.int64)


E2M1 = np.array([0.0, 0.5, 1.0, 1.5, 2.0, 3.0, 4.0, 6.0, -0.0, -0.5, -1.0, -1.5, -2.0, -3.0, -4.0, -6.0])


def pack_weight(w, fmt):
    k, n = w.shape
    w = f64(np.asarray(w, np.float32).astype(ml_dtypes.bfloat16)).reshape(k // 32, 32, n)
    amax = np.abs(w).max(1)
    if fmt == "e4m3":
        byte = np.frexp(amax)[1] - 1 + 127 - 7
    else:
        mant, ex = np.frexp(amax / 6.0)
        byte = np.where(mant > 0.5, ex, ex - 1) + 127
    byte = np.clip(np.where(amax > 0, byte, 1), 1, 254)
    scaled = (w * np.exp2(127.0 - byte)[:, None, :]).reshape(k, n).astype(np.float32)
    by_word = np.ascontiguousarray(scaled.reshape(k // 512, 128, 4, n).transpose(0, 1, 3, 2))
    if fmt == "e4m3":
        words = by_word.astype(ml_dtypes.float8_e4m3fn).view(np.uint8)
    else:
        c = by_word.astype(ml_dtypes.float4_e2m1fn).view(np.uint8) & 0xF
        words = (c[..., 0::2] | (c[..., 1::2] << 4)).reshape(k // 512, 128, 2 * n)
    return np.ascontiguousarray(words), np.ascontiguousarray(byte.astype(np.uint8).reshape(k // 512, 16, n))


def unpack_weight(words, scales, fmt):
    g, _, n = scales.shape
    words = np.ascontiguousarray(words).reshape(g, 128, n, -1)
    if fmt == "e4m3":
        vals = words.view(ml_dtypes.float8_e4m3fn).astype(np.float64)
    else:
        nib = np.empty((g, 128, n, 4), np.uint8)
        nib[..., 0::2] = words & 0xF
        nib[..., 1::2] = words >> 4
        vals = E2M1[nib]
    vals = vals * np.repeat(np.exp2(scales.astype(np.float64) - 127.0), 8, axis=1)[..., None]
    return vals.transpose(0, 1, 3, 2).reshape(g * 512, n)


def gelu(v):
    return 0.5 * v * (1.0 + np.tanh(np.sqrt(2.0 / np.pi) * (v + 0.044715 * v**3)))


def striped8(idx):
    return np.concatenate([v.reshape(-1, 16).T for v in idx]).astype(np.uint16)


def unstriped8(offs):
    return np.stack([offs[16 * g:16 * g + 16].T.reshape(-1) for g in range(8)]).astype(np.int64)


def runs(v, idx8):
    k = np.arange(v.shape[0])
    return v[k[:, None], idx8[k % 512 // 64]]


K, H, T, S, P = 1536, 1024, 2048, 1024, 512


def setup_inputs():
    n = np.random.standard_normal
    s = mx_kscale(K)[:, None]
    u = mx_kscale(H)[:, None]
    d = {}
    d["tab_words"], d["tab_scales"] = pack_weight(n((K, T)) * s, "e4m3")
    d["offs"] = striped8(np.stack([np.random.permutation(T)[:S] for _ in range(8)]))
    d["pos1"] = striped(np.random.permutation(S)[:P])
    d["pos2"] = striped(np.random.permutation(S)[:P])
    d["w1"] = (1.5 * n((K, H)) / (s * K ** 0.5)).astype(np.float32)
    d["gain"] = np.random.uniform(1.2, 1.7, H).astype(np.float32)
    d["carry"] = (u[:, 0] * np.exp(0.3 * n(H))).astype(np.float32)
    d["w2_words"], d["w2_scales"] = pack_weight(1.7 * n((H, H)) / (u * H ** 0.5), "e2m1")
    return d


def reference(tab_words, tab_scales, offs, pos1, pos2, w1, gain, carry, w2_words, w2_scales):
    v = runs(unpack_weight(tab_words, tab_scales, "e4m3"), unstriped8(offs))
    a = mxq(f64(w1), 0, "e4m3").T @ v
    h = f64(gain)[:, None] * np.tanh(a)
    kept = h[:, unstriped(pos1)] * h[:, unstriped(pos2)]
    x = f64(carry)[:, None] * np.sin(kept)
    w2 = unpack_weight(w2_words, w2_scales, "e2m1")
    y = w2.T @ mxq(x, 0, "e4m3")
    return kept + y

@@ -1,0 +1,328 @@
+from contextlib import ExitStack
+
+import concourse.mybir as mybir
+
+K, H, T, S, M = 1536, 1024, 2048, 1024, 512
+FLOPS = 2 * K * H * S + 2 * H * H * M
+
+F32 = mybir.dt.float32
+BF16 = mybir.dt.bfloat16
+I32 = mybir.dt.int32
+U32 = mybir.dt.uint32
+U16 = mybir.dt.uint16
+U8 = mybir.dt.uint8
+FP8X4 = mybir.dt.float8_e4m3fn_x4
+FP4X4 = mybir.dt.float4_e2m1fn_x4
+ACT = mybir.ActivationFunctionType
+MULT = mybir.AluOpType.mult
+ADD = mybir.AluOpType.add
+
+P = 128
+PACK = 4
+PASS = P * PACK
+BANK = 512
+K_PASSES = K // PASS
+BLOCKS = H // PASS
+HALF = M // 2
+CHUNK = 128
+PLANE_ROW = (0, 8, 4)
+
+
+def tile_list_hatchery_turning_outlooks_kernel(
+    tc, tab_words, tab_scales, offs, pos1, pos2, w1, gain, carry, w2_words, w2_scales, out
+):
+    nc = tc.nc
+    with ExitStack() as ctx:
+        keep = ctx.enter_context(tc.tile_pool(name="keep", bufs=1))
+        psum = ctx.enter_context(tc.psum_pool(name="psum", bufs=1))
+
+        def sb(name, shape, dtype):
+            return keep.tile(shape, dtype, name=name, align_bytes=64)
+
+        def bank(i, stage):
+            return psum.tile([P, BANK], F32, name="%s_bank%d" % (stage, i), tag="bank%d" % i)
+
+        offs_t = keep.tile([P, S // 16], U16, name="offs_t")
+        pos1_t = keep.tile([P, M // 16], U16, name="pos1_t")
+        pos2_t = keep.tile([P, M // 16], U16, name="pos2_t")
+
+        scale_window = sb("scale_window", [P, T], U8)
+        scale_picked = sb("scale_picked", [P, S], U8)
+        v_scales = sb("v_scales", [P, S], U8)
+        w2s_raw = sb("w2s_raw", [P, BLOCKS, H], U8)
+        warm = sb("warm", [P, 2], F32)
+
+        nc.gpsimd.memset(scale_window[:].bitcast(I32), 0)
+        nc.gpsimd.memset(v_scales[:].bitcast(I32), 0)
+        nc.gpsimd.memset(warm[:, 0:1], 0.0)
+        nc.gpsimd.memset(w2s_raw[:].rearrange("p a c -> p (a c)").bitcast(I32), 0)
+
+        tab = [sb("tab%d" % a, [P, T], I32) for a in range(K_PASSES)]
+
+        def load_tab(a):
+            nc.sync.dma_start(tab[a][:], tab_words[a].rearrange("p t i -> p (t i)").bitcast(I32))
+
+        nc.sync.dma_start(offs_t[:], offs)
+        load_tab(0)
+        rows = tab_scales.rearrange("a (g e) t -> e g a t", e=2)
+        for e in range(2):
+            nc.sync.dma_start(scale_window[e:P:8, :].bitcast(I32), rows[e][:, 0:2, :].bitcast(I32))
+        for e in range(2):
+            nc.sync.dma_start(scale_window[4 + e : P : 16, :].bitcast(I32), rows[e][:, 2, :].bitcast(I32))
+        nc.scalar.activation(warm[:, 1:2], warm[:, 0:1], ACT.Silu)
+
+
+        raw = {}
+
+        def load_w1(b, a, q0, q1):
+            raw[b, a, q0] = sb("raw%d_%d_%d" % (b, a, q0), [P, PACK, PACK * (q1 - q0)], F32)
+            src = w1[PASS * a : PASS * (a + 1), PASS * b + PACK * q0 : PASS * b + PACK * q1]
+            nc.sync.dma_start(raw[b, a, q0][:], src.rearrange("(p j) c -> p j c", j=PACK))
+
+        gain_t = sb("gain_t", [P, BLOCKS, PACK], F32)
+        carry_t = sb("carry_t", [P, BLOCKS, PACK], F32)
+        gain2 = sb("gain2", [P, BLOCKS, PACK], F32)
+        w2w_raw = sb("w2w_raw", [P, BLOCKS, 2 * H], U8)
+        load_w1(0, 0, 0, P)
+        load_tab(1)
+        load_tab(2)
+        load_w1(0, 1, 0, P // 2)
+        nc.vector.tensor_copy(scale_picked[:], scale_window[:].indirect(offs_t[:]))
+        for e in range(2):
+            nc.scalar.dma_start(v_scales[e:P:4, :].bitcast(I32), scale_picked[e:P:4, :].bitcast(I32))
+        for e in range(2):
+            nc.scalar.dma_start(
+                v_scales[2 + e : 2 + e + P - 16 : 4, :].bitcast(I32), scale_picked[16 + e : P : 4, :].bitcast(I32)
+            )
+        load_w1(0, 1, P // 2, P)
+        for d in range(4):
+            nc.sync.dma_start(
+                w2s_raw[32 * d : 32 * d + 4, :, :].bitcast(I32),
+                w2_scales[:, 4 * d : 4 * d + 4, :].rearrange("a r c -> r a c").bitcast(I32),
+            )
+        load_w1(0, 2, 0, P // 2)
+        load_w1(0, 2, P // 2, P)
+        nc.sync.dma_start(pos1_t[:], pos1)
+        nc.sync.dma_start(pos2_t[:], pos2)
+        nc.sync.dma_start(w2w_raw[:].bitcast(I32), w2_words.rearrange("a p c -> p a c").bitcast(I32))
+        load_w1(1, 0, 0, P)
+        nc.sync.dma_start(gain_t[:], gain.rearrange("(b p t) -> p b t", b=BLOCKS, t=PACK))
+        nc.sync.dma_start(carry_t[:], carry.rearrange("(b p t) -> p b t", b=BLOCKS, t=PACK))
+        load_w1(1, 1, 0, P)
+        load_w1(1, 2, 0, P)
+
+        v_words = [sb("v_words%d" % a, [P, S], U32) for a in range(K_PASSES)]
+
+        def gather_tab(a):
+            nc.vector.tensor_copy(v_words[a][:], tab[a][:].bitcast(U32).indirect(offs_t[:]))
+
+        grouped = {}
+        w1_codes = {}
+        w1_scales = {}
+        for b in range(BLOCKS):
+            for a in range(K_PASSES):
+                grouped[b, a] = sb("grouped%d_%d" % (b, a), [P, PASS * PACK // 2], F32)
+                w1_codes[b, a] = sb("w1_codes%d_%d" % (b, a), [P, PASS], U32)
+                w1_scales[b, a] = sb("w1_scales%d_%d" % (b, a), [P, PASS], U8)
+
+        def deal_w1(copy, b, a, q0, q1):
+            dst = grouped[b, a][:].bitcast(BF16).rearrange("p (t q j) -> p q j t", t=PACK, j=PACK)
+            copy(dst[:, q0:q1], raw[b, a, q0][:].rearrange("p j (q t) -> p q j t", t=PACK))
+
+        def quantize_w1(b, a, t0, t1):
+            nc.vector.quantize_mx(
+                out=w1_codes[b, a][:, P * t0 : P * t1].bitcast(FP8X4),
+                scales=w1_scales[b, a][:, P * t0 : P * t1],
+                in_=grouped[b, a][:].bitcast(BF16)[:, PASS * t0 : PASS * t1],
+            )
+
+        acc = {}
+
+        def first_pass(b, a, t):
+            for c in range(S // BANK):
+                if a == 0:
+                    acc[b, t, c] = bank(2 * t + c, "first%d" % b)
+                nc.tensor.matmul_mx(
+                    out=acc[b, t, c][:],
+                    lhsT=w1_codes[b, a][:, P * t : P * (t + 1)].bitcast(FP8X4),
+                    lhsT_scale=w1_scales[b, a][:, P * t : P * (t + 1)],
+                    rhs=v_words[a][:, BANK * c : BANK * (c + 1)].bitcast(FP8X4),
+                    rhs_scale=v_scales[PLANE_ROW[a] : P, BANK * c : BANK * (c + 1)],
+                    start=(a == 0),
+                    stop=(a == K_PASSES - 1),
+                )
+
+        th = {}
+
+        def tanh_rows(b, t):
+            th[b, t] = sb("th%d_%d" % (b, t), [P, S], F32)
+            for c in range(S // BANK):
+                nc.scalar.activation(th[b, t][:, BANK * c : BANK * (c + 1)], acc[b, t, c][:], ACT.Tanh)
+
+        gather_tab(0)
+        deal_w1(nc.scalar.copy, 0, 0, 0, P)
+        gather_tab(1)
+        quantize_w1(0, 0, 0, PACK)
+        gather_tab(2)
+        deal_w1(nc.scalar.copy, 0, 1, 0, P // 2)
+        deal_w1(nc.scalar.copy, 0, 1, P // 2, P)
+        deal_w1(nc.scalar.copy, 0, 2, 0, P // 2)
+        quantize_w1(0, 1, 0, PACK)
+        deal_w1(nc.vector.tensor_copy, 0, 2, P // 2, P)
+        for t0, t1 in ((0, 1), (1, 2), (2, 4)):
+            quantize_w1(0, 2, t0, t1)
+            for t in range(t0, t1):
+                for a in range(K_PASSES):
+                    first_pass(0, a, t)
+        nc.vector.tensor_tensor(gain2[:], gain_t[:], gain_t[:], MULT)
+
+        w2w = sb("w2w", [P, BLOCKS * 2 * H], U8)
+        w2s = sb("w2s", [P, BLOCKS * H], U8)
+        nc.vector.tensor_copy(
+            w2w[:].bitcast(U16).rearrange("p (k t c i) -> p k c t i", t=PACK, c=16, i=8),
+            w2w_raw[:].rearrange("p a c -> p (a c)").bitcast(U16).rearrange("p (k c i t) -> p k c t i", t=PACK, c=16, i=8),
+        )
+        nc.vector.tensor_copy(
+            w2s[:].rearrange("p (k t c i) -> p k c t i", t=PACK, c=8, i=16),
+            w2s_raw[:].rearrange("p a c -> p (a c)").rearrange("p (k c i t) -> p k c t i", t=PACK, c=8, i=16),
+        )
+
+        def pick_early(dst, b, t, m0, m1):
+            nc.vector.tensor_copy(dst, th[b, t][:].indirect(pos1_t[:, m0 // 16 : m1 // 16]))
+
+        def times_late(dst, early, b, t, m0, m1):
+            nc.vector.tensor_tensor(dst, th[b, t][:].indirect(pos2_t[:, m0 // 16 : m1 // 16]), early, MULT)
+
+        early = sb("early", [P, 2, M], F32)
+        prod0 = sb("prod0", [P, PACK - 1, M], F32)
+        early0 = [early[:, 0, :], early[:, 1, :], grouped[1, 0][:, 0:M], grouped[1, 1][:, 0:M]]
+        prod = {(0, t): prod0[:, t, :] for t in range(PACK - 1)}
+        prod[0, PACK - 1] = grouped[1, 2][:, 0:M]
+
+        tanh_rows(0, 0)
+        probe = sb("probe", [P, 2], F32)
+        nc.gpsimd.tensor_copy(probe[:, 0:1], th[0, 0][:, S - 1 : S])
+        tanh_rows(0, 1)
+        deal_w1(nc.scalar.copy, 1, 0, 0, P)
+        tanh_rows(0, 2)
+        deal_w1(nc.scalar.copy, 1, 1, 0, P)
+        tanh_rows(0, 3)
+        deal_w1(nc.scalar.copy, 1, 2, 0, P)
+        for t in range(PACK):
+            if t >= 2:
+                quantize_w1(1, t - 2, 0, PACK)
+            pick_early(early0[t], 0, t, 0, M)
+            if t == PACK - 1:
+                quantize_w1(1, 2, 0, PACK)
+            times_late(prod[0, t], early0[t], 0, t, 0, M)
+        for t in range(PACK):
+            for a in range(K_PASSES):
+                first_pass(1, a, t)
+            tanh_rows(1, t)
+
+        sines = raw[1, 2, 0]
+
+        def sine_rows(rows_bf, src, b, t, width):
+            s = sines[:, t % 2, 0:width]
+            nc.scalar.activation(s, src, ACT.Sin, scale=gain2[:, b, t : t + 1])
+            nc.scalar.activation(rows_bf[:, width * t : width * (t + 1)], s, ACT.Copy, scale=carry_t[:, b, t : t + 1])
+
+        def weave(copy, woven_bf, rows_bf):
+            copy(
+                woven_bf.rearrange("p (c i t) -> p c t i", i=4, t=PACK),
+                rows_bf.rearrange("p (t c i) -> p c t i", i=4, t=PACK),
+            )
+
+        def quantize_x(name, woven_bf, width):
+            codes = sb(name + "_codes", [P, width], U32)
+            scales = sb(name + "_scales", [P, width], U8)
+            nc.vector.quantize_mx(out=codes[:].bitcast(FP8X4), scales=scales[:], in_=woven_bf)
+            return codes, scales
+
+        rows0 = sb("rows0", [P, PACK * M // 2], F32)
+        woven0 = sb("woven0", [P, PACK * M // 2], F32)
+        for t in range(PACK):
+            sine_rows(rows0[:].bitcast(BF16), prod[0, t], 0, t, M)
+
+        prod1 = [sb("prod1_%d" % h, [P, PACK, HALF], F32) for h in range(2)]
+        rows1 = [sb("rows1_%d" % h, [P, PACK * HALF], BF16) for h in range(2)]
+        woven1 = [sb("woven1_%d" % h, [P, PACK * HALF // 2], F32) for h in range(2)]
+        ring = [early[:, 0, 0:HALF], early[:, 1, 0:HALF]]
+
+        y = {}
+
+        def second_pass(h, a, codes, scales, m0):
+            for i in range(4):
+                if a == 0:
+                    y[h, i] = bank(4 * h + i, "second")
+                for n in range(2):
+                    col = H * a + P * (2 * i + n)
+                    for c in range(HALF // CHUNK):
+                        nc.tensor.matmul_mx(
+                            out=y[h, i][:, HALF * n + CHUNK * c : HALF * n + CHUNK * (c + 1)],
+                            lhsT=w2w[:, 2 * col : 2 * (col + P)].bitcast(FP4X4),
+                            lhsT_scale=w2s[:, col : col + P],
+                            rhs=codes[:, m0 + CHUNK * c : m0 + CHUNK * (c + 1)].bitcast(FP8X4),
+                            rhs_scale=scales[:, m0 + CHUNK * c : m0 + CHUNK * (c + 1)],
+                            start=(a == 0 and n == 0 and c == 0),
+                            stop=(a == BLOCKS - 1 and n == 1 and c == HALF // CHUNK - 1),
+                        )
+
+        for t in range(PACK + 1):
+            if t < PACK:
+                pick_early(ring[t % 2], 1, t, 0, HALF)
+            if t > 0:
+                times_late(prod1[0][:, t - 1, :], ring[(t - 1) % 2], 1, t - 1, 0, HALF)
+        for t in range(PACK):
+            sine_rows(rows1[0][:], prod1[0][:, t, :], 1, t, HALF)
+        weave(nc.scalar.copy, woven1[0][:].bitcast(BF16), rows1[0][:])
+
+        early1 = [ring[0], ring[1], rows0[:, 0:HALF], woven0[:, 0:HALF]]
+        last = [prod1[1][:, 0, :], prod1[1][:, 1, :], prod1[1][:, 2, :], woven1[0][:, 0:HALF]]
+        pick_early(early1[0], 1, 0, HALF, M)
+        pick_early(early1[1], 1, 1, HALF, M)
+        times_late(last[0], early1[0], 1, 0, HALF, M)
+        weave(nc.vector.tensor_copy, woven0[:].bitcast(BF16), rows0[:].bitcast(BF16))
+        pick_early(early1[2], 1, 2, HALF, M)
+        times_late(last[1], early1[1], 1, 1, HALF, M)
+        x0 = quantize_x("x0", woven0[:].bitcast(BF16), M)
+        pick_early(early1[3], 1, 3, HALF, M)
+        times_late(last[2], early1[2], 1, 2, HALF, M)
+        x10 = quantize_x("x10", woven1[0][:].bitcast(BF16), HALF)
+        times_late(last[3], early1[3], 1, 3, HALF, M)
+        nc.gpsimd.tensor_copy(probe[:, 1:2], last[3][:, 0:1])
+        second_pass(0, 0, x0[0], x0[1], 0)
+        second_pass(0, 1, x10[0], x10[1], 0)
+        second_pass(1, 0, x0[0], x0[1], HALF)
+        for t in range(PACK):
+            sine_rows(rows1[1][:], last[t], 1, t, HALF)
+        weave(nc.scalar.copy, woven1[1][:].bitcast(BF16), rows1[1][:])
+
+        out_rows = out.rearrange("(b p t) m -> b p t m", b=BLOCKS, t=PACK)
+
+        def finish(h, banks):
+            for i in banks:
+                b = i // 2
+                if (h, i) == (0, 3):
+                    res = woven1[1][:].rearrange("p (n m) -> p n m", n=2)
+                else:
+                    res = sb("res%d_%d" % (h, i), [P, 2, HALF], F32)
+                for n in range(2):
+                    t = 2 * (i % 2) + n
+                    if b == 0:
+                        src = prod[0, t][:, HALF * h : HALF * (h + 1)]
+                    elif h == 0:
+                        src = prod1[0][:, t, :]
+                    else:
+                        src = last[t]
+                    nc.vector.scalar_tensor_tensor(
+                        res[:, n, :], src, gain2[:, b, t : t + 1], y[h, i][:, HALF * n : HALF * (n + 1)], MULT, ADD
+                    )
+                t0 = 2 * (i % 2)
+                nc.sync.dma_start(out_rows[b][:, t0 : t0 + 2, HALF * h : HALF * (h + 1)], res[:])
+
+        finish(0, range(3))
+        x11 = quantize_x("x11", woven1[1][:].bitcast(BF16), HALF)
+        second_pass(1, 1, x11[0], x11[1], 0)
+        finish(0, range(3, 4))
+        finish(1, range(4))

@@ -26,6 +26,8 @@ BLOCKS = H // PASS
 HALF = M // 2
 CHUNK = 128
 PLANE_ROW = (0, 8, 4)
+HEAD_SHARE = 84
+TURN_SHARE = 40
 
 
 def tile_list_hatchery_turning_outlooks_kernel(
@@ -36,8 +38,8 @@ def tile_list_hatchery_turning_outlooks_kernel(
         keep = ctx.enter_context(tc.tile_pool(name="keep", bufs=1))
         psum = ctx.enter_context(tc.psum_pool(name="psum", bufs=1))
 
-        def sb(name, shape, dtype):
-            return keep.tile(shape, dtype, name=name, align_bytes=64)
+        def sb(name, shape, dtype, after=None):
+            return keep.tile(shape, dtype, name=name, tag=after or name, align_bytes=64)
 
         def bank(i, stage):
             return psum.tile([P, BANK], F32, name="%s_bank%d" % (stage, i), tag="bank%d" % i)
@@ -53,9 +55,9 @@ def tile_list_hatchery_turning_outlooks_kernel(
         warm = sb("warm", [P, 2], F32)
 
         nc.gpsimd.memset(scale_window[:].bitcast(I32), 0)
-        nc.gpsimd.memset(v_scales[:].bitcast(I32), 0)
         nc.gpsimd.memset(warm[:, 0:1], 0.0)
-        nc.gpsimd.memset(w2s_raw[:].rearrange("p a c -> p (a c)").bitcast(I32), 0)
+        nc.vector.memset(v_scales[:].bitcast(I32), 0)
+        nc.vector.memset(w2s_raw[:].rearrange("p a c -> p (a c)").bitcast(I32), 0)
 
         tab = [sb("tab%d" % a, [P, T], I32) for a in range(K_PASSES)]
 
@@ -74,42 +76,22 @@ def tile_list_hatchery_turning_outlooks_kernel(
 
         raw = {}
 
-        def load_w1(b, a, q0, q1):
-            raw[b, a, q0] = sb("raw%d_%d_%d" % (b, a, q0), [P, PACK, PACK * (q1 - q0)], F32)
-            src = w1[PASS * a : PASS * (a + 1), PASS * b + PACK * q0 : PASS * b + PACK * q1]
-            nc.sync.dma_start(raw[b, a, q0][:], src.rearrange("(p j) c -> p j c", j=PACK))
+        def load_w1(b, a, after=None):
+            raw[b, a] = sb("raw%d_%d" % (b, a), [P, PACK, PASS], F32, after)
+            src = w1[PASS * a : PASS * (a + 1), PASS * b : PASS * (b + 1)]
+            nc.sync.dma_start(raw[b, a][:], src.rearrange("(p j) c -> p j c", j=PACK))
 
-        gain_t = sb("gain_t", [P, BLOCKS, PACK], F32)
-        carry_t = sb("carry_t", [P, BLOCKS, PACK], F32)
-        gain2 = sb("gain2", [P, BLOCKS, PACK], F32)
-        w2w_raw = sb("w2w_raw", [P, BLOCKS, 2 * H], U8)
-        load_w1(0, 0, 0, P)
-        load_tab(1)
-        load_tab(2)
-        load_w1(0, 1, 0, P // 2)
-        nc.vector.tensor_copy(scale_picked[:], scale_window[:].indirect(offs_t[:]))
-        for e in range(2):
-            nc.scalar.dma_start(v_scales[e:P:4, :].bitcast(I32), scale_picked[e:P:4, :].bitcast(I32))
-        for e in range(2):
-            nc.scalar.dma_start(
-                v_scales[2 + e : 2 + e + P - 16 : 4, :].bitcast(I32), scale_picked[16 + e : P : 4, :].bitcast(I32)
-            )
-        load_w1(0, 1, P // 2, P)
+        nc.sync.dma_start(pos1_t[:], pos1)
+        nc.sync.dma_start(pos2_t[:], pos2)
         for d in range(4):
-            nc.sync.dma_start(
+            nc.gpsimd.dma_start(
                 w2s_raw[32 * d : 32 * d + 4, :, :].bitcast(I32),
                 w2_scales[:, 4 * d : 4 * d + 4, :].rearrange("a r c -> r a c").bitcast(I32),
             )
-        load_w1(0, 2, 0, P // 2)
-        load_w1(0, 2, P // 2, P)
-        nc.sync.dma_start(pos1_t[:], pos1)
-        nc.sync.dma_start(pos2_t[:], pos2)
-        nc.sync.dma_start(w2w_raw[:].bitcast(I32), w2_words.rearrange("a p c -> p a c").bitcast(I32))
-        load_w1(1, 0, 0, P)
-        nc.sync.dma_start(gain_t[:], gain.rearrange("(b p t) -> p b t", b=BLOCKS, t=PACK))
-        nc.sync.dma_start(carry_t[:], carry.rearrange("(b p t) -> p b t", b=BLOCKS, t=PACK))
-        load_w1(1, 1, 0, P)
-        load_w1(1, 2, 0, P)
+        load_w1(0, 0)
+        load_tab(1)
+        load_tab(2)
+        load_w1(0, 1)
 
         v_words = [sb("v_words%d" % a, [P, S], U32) for a in range(K_PASSES)]
 
@@ -126,8 +108,9 @@ def tile_list_hatchery_turning_outlooks_kernel(
                 w1_scales[b, a] = sb("w1_scales%d_%d" % (b, a), [P, PASS], U8)
 
         def deal_w1(copy, b, a, q0, q1):
-            dst = grouped[b, a][:].bitcast(BF16).rearrange("p (t q j) -> p q j t", t=PACK, j=PACK)
-            copy(dst[:, q0:q1], raw[b, a, q0][:].rearrange("p j (q t) -> p q j t", t=PACK))
+            dst = grouped[b, a][:].bitcast(BF16).rearrange("p (u v q j) -> p u q j v", u=2, v=2, j=PACK)
+            src = raw[b, a][:].rearrange("p j (q u v) -> p u q j v", u=2, v=2)
+            copy(dst[:, :, q0:q1], src[:, :, q0:q1])
 
         def quantize_w1(b, a, t0, t1):
             nc.vector.quantize_mx(
@@ -141,7 +124,7 @@ def tile_list_hatchery_turning_outlooks_kernel(
         def first_pass(b, a, t):
             for c in range(S // BANK):
                 if a == 0:
-                    acc[b, t, c] = bank(2 * t + c, "first%d" % b)
+                    acc[b, t, c] = bank(4 * b + 2 * (t % 2) + c, "first%d_%d" % (b, t))
                 nc.tensor.matmul_mx(
                     out=acc[b, t, c][:],
                     lhsT=w1_codes[b, a][:, P * t : P * (t + 1)].bitcast(FP8X4),
@@ -152,6 +135,10 @@ def tile_list_hatchery_turning_outlooks_kernel(
                     stop=(a == K_PASSES - 1),
                 )
 
+        def first_product(b, t):
+            for a in range(K_PASSES):
+                first_pass(b, a, t)
+
         th = {}
 
         def tanh_rows(b, t):
@@ -160,24 +147,40 @@ def tile_list_hatchery_turning_outlooks_kernel(
                 nc.scalar.activation(th[b, t][:, BANK * c : BANK * (c + 1)], acc[b, t, c][:], ACT.Tanh)
 
         gather_tab(0)
+        nc.vector.tensor_copy(scale_picked[:], scale_window[:].indirect(offs_t[:]))
+        for e in range(2):
+            nc.sync.dma_start(v_scales[e:P:4, :].bitcast(I32), scale_picked[e:P:4, :].bitcast(I32))
+        for e in range(2):
+            nc.sync.dma_start(
+                v_scales[2 + e : 2 + e + P - 16 : 4, :].bitcast(I32), scale_picked[16 + e : P : 4, :].bitcast(I32)
+            )
+        load_w1(0, 2, after="scale_window")
         deal_w1(nc.scalar.copy, 0, 0, 0, P)
         gather_tab(1)
+        w2w_raw = sb("w2w_raw", [P, BLOCKS, 2 * H], U8, after="tab1")
+        nc.sync.dma_start(w2w_raw[:].bitcast(I32), w2_words.rearrange("a p c -> p a c").bitcast(I32))
         quantize_w1(0, 0, 0, PACK)
         gather_tab(2)
-        deal_w1(nc.scalar.copy, 0, 1, 0, P // 2)
-        deal_w1(nc.scalar.copy, 0, 1, P // 2, P)
-        deal_w1(nc.scalar.copy, 0, 2, 0, P // 2)
-        quantize_w1(0, 1, 0, PACK)
-        deal_w1(nc.vector.tensor_copy, 0, 2, P // 2, P)
+        load_w1(1, 0, after="grouped0_0")
+        gain_t = sb("gain_t", [P, BLOCKS, PACK], F32, after="scale_picked")
+        carry_t = sb("carry_t", [P, BLOCKS, PACK], F32, after="raw0_0")
+        gain2 = sb("gain2", [P, BLOCKS, PACK], F32)
+        nc.sync.dma_start(gain_t[:], gain.rearrange("(b p t) -> p b t", b=BLOCKS, t=PACK))
+        nc.sync.dma_start(carry_t[:], carry.rearrange("(b p t) -> p b t", b=BLOCKS, t=PACK))
+        deal_w1(nc.scalar.copy, 0, 1, 0, P)
+        load_w1(1, 1, after="raw0_1")
+        deal_w1(nc.vector.tensor_copy, 0, 2, 0, HEAD_SHARE)
+        deal_w1(nc.scalar.copy, 0, 2, HEAD_SHARE, P)
+        load_w1(1, 2, after="scale_window")
         for t0, t1 in ((0, 1), (1, 2), (2, 4)):
+            quantize_w1(0, 1, t0, t1)
             quantize_w1(0, 2, t0, t1)
-            for t in range(t0, t1):
-                for a in range(K_PASSES):
-                    first_pass(0, a, t)
-        nc.vector.tensor_tensor(gain2[:], gain_t[:], gain_t[:], MULT)
+            if t0 < 2:
+                first_product(0, t0)
+        nc.scalar.activation(gain2[:], gain_t[:], ACT.Square)
 
         w2w = sb("w2w", [P, BLOCKS * 2 * H], U8)
-        w2s = sb("w2s", [P, BLOCKS * H], U8)
+        w2s = sb("w2s", [P, BLOCKS * H], U8, after="tab2")
         nc.vector.tensor_copy(
             w2w[:].bitcast(U16).rearrange("p (k t c i) -> p k c t i", t=PACK, c=16, i=8),
             w2w_raw[:].rearrange("p a c -> p (a c)").bitcast(U16).rearrange("p (k c i t) -> p k c t i", t=PACK, c=16, i=8),
@@ -187,45 +190,81 @@ def tile_list_hatchery_turning_outlooks_kernel(
             w2s_raw[:].rearrange("p a c -> p (a c)").rearrange("p (k c i t) -> p k c t i", t=PACK, c=8, i=16),
         )
 
-        def pick_early(dst, b, t, m0, m1):
-            nc.vector.tensor_copy(dst, th[b, t][:].indirect(pos1_t[:, m0 // 16 : m1 // 16]))
+        def half(ap, h):
+            return ap[:, HALF * h : HALF * (h + 1)]
 
-        def times_late(dst, early, b, t, m0, m1):
-            nc.vector.tensor_tensor(dst, th[b, t][:].indirect(pos2_t[:, m0 // 16 : m1 // 16]), early, MULT)
+        def pick_early(dst, b, t, h):
+            nc.vector.tensor_copy(dst, th[b, t][:].indirect(pos1_t[:, 16 * h : 16 * (h + 1)]))
 
-        early = sb("early", [P, 2, M], F32)
-        prod0 = sb("prod0", [P, PACK - 1, M], F32)
-        early0 = [early[:, 0, :], early[:, 1, :], grouped[1, 0][:, 0:M], grouped[1, 1][:, 0:M]]
-        prod = {(0, t): prod0[:, t, :] for t in range(PACK - 1)}
-        prod[0, PACK - 1] = grouped[1, 2][:, 0:M]
+        def times_late(dst, early_half, b, t, h):
+            nc.vector.tensor_tensor(dst, th[b, t][:].indirect(pos2_t[:, 16 * h : 16 * (h + 1)]), early_half, MULT)
+
+        early_buf = sb("early_buf", [P, 2, M], F32)
+        prod_buf = sb("prod_buf", [P, 6, M], F32)
+        rows0 = sb("rows0", [P, PACK * M // 2], F32)
+        woven0 = sb("woven0", [P, PACK * M // 2], F32)
+        rows1 = sb("rows1", [P, 2, PACK, HALF], BF16)
+        woven1 = [sb("woven1_%d" % h, [P, PACK * HALF // 2], F32) for h in range(2)]
+
+        early = {}
+        prod = {}
+        for h in range(2):
+            for t in range(2):
+                early[0, t, h] = half(early_buf[:, t, :], h)
+                early[0, t + 2, h] = half(grouped[1, t][:, 0:M], h)
+                early[1, t, h] = half(early_buf[:, t, :], h)
+                early[1, t + 2, h] = half(early_buf[:, t, :], h)
+                prod[1, t, h] = half(prod_buf[:, 3 + t, :], h)
+            for t in range(3):
+                prod[0, t, h] = half(prod_buf[:, t, :], h)
+            prod[0, 3, h] = half(grouped[1, 2][:, 0:M], h)
+        early[1, 3, 1] = woven0[:, 0:HALF]
+        prod[1, 2, 0] = prod_buf[:, 5, 0:HALF]
+        prod[1, 3, 0] = rows0[:, 0:HALF]
+        prod[1, 2, 1] = woven0[:, HALF:M]
+        prod[1, 3, 1] = woven1[0][:, 0:HALF]
+
+        def picks(b, t, halves):
+            for h in halves:
+                pick_early(early[b, t, h], b, t, h)
+
+        def products(b, t, halves):
+            for h in halves:
+                times_late(prod[b, t, h], early[b, t, h], b, t, h)
 
         tanh_rows(0, 0)
         probe = sb("probe", [P, 2], F32)
         nc.gpsimd.tensor_copy(probe[:, 0:1], th[0, 0][:, S - 1 : S])
+        first_product(0, 2)
         tanh_rows(0, 1)
+        first_product(0, 3)
         deal_w1(nc.scalar.copy, 1, 0, 0, P)
         tanh_rows(0, 2)
         deal_w1(nc.scalar.copy, 1, 1, 0, P)
         tanh_rows(0, 3)
-        deal_w1(nc.scalar.copy, 1, 2, 0, P)
+        deal_w1(nc.vector.tensor_copy, 1, 2, 0, TURN_SHARE)
+        deal_w1(nc.scalar.copy, 1, 2, TURN_SHARE, P)
         for t in range(PACK):
             if t >= 2:
                 quantize_w1(1, t - 2, 0, PACK)
-            pick_early(early0[t], 0, t, 0, M)
+            picks(0, t, range(2))
             if t == PACK - 1:
-                quantize_w1(1, 2, 0, PACK)
-            times_late(prod[0, t], early0[t], 0, t, 0, M)
+                quantize_w1(1, 2, 0, 2)
+                quantize_w1(1, 2, 2, PACK)
+            products(0, t, range(2))
         for t in range(PACK):
-            for a in range(K_PASSES):
-                first_pass(1, a, t)
+            first_product(1, t)
             tanh_rows(1, t)
 
-        sines = raw[1, 2, 0]
+        sines = raw[1, 2]
 
-        def sine_rows(rows_bf, src, b, t, width):
+        def sine_rows(dst, src, b, t):
+            width = src.shape[1]
             s = sines[:, t % 2, 0:width]
             nc.scalar.activation(s, src, ACT.Sin, scale=gain2[:, b, t : t + 1])
-            nc.scalar.activation(rows_bf[:, width * t : width * (t + 1)], s, ACT.Copy, scale=carry_t[:, b, t : t + 1])
+            if width == M:
+                s = s.rearrange("p (h m) -> p h m", h=2)
+            nc.scalar.activation(dst, s, ACT.Copy, scale=carry_t[:, b, t : t + 1])
 
         def weave(copy, woven_bf, rows_bf):
             copy(
@@ -239,90 +278,79 @@ def tile_list_hatchery_turning_outlooks_kernel(
             nc.vector.quantize_mx(out=codes[:].bitcast(FP8X4), scales=scales[:], in_=woven_bf)
             return codes, scales
 
-        rows0 = sb("rows0", [P, PACK * M // 2], F32)
-        woven0 = sb("woven0", [P, PACK * M // 2], F32)
+        rows0_bf = rows0[:].bitcast(BF16).rearrange("p (t h m) -> p t h m", t=PACK, h=2)
         for t in range(PACK):
-            sine_rows(rows0[:].bitcast(BF16), prod[0, t], 0, t, M)
-
-        prod1 = [sb("prod1_%d" % h, [P, PACK, HALF], F32) for h in range(2)]
-        rows1 = [sb("rows1_%d" % h, [P, PACK * HALF], BF16) for h in range(2)]
-        woven1 = [sb("woven1_%d" % h, [P, PACK * HALF // 2], F32) for h in range(2)]
-        ring = [early[:, 0, 0:HALF], early[:, 1, 0:HALF]]
+            whole = prod_buf[:, t, :] if t < 3 else grouped[1, 2][:, 0:M]
+            sine_rows(rows0_bf[:, t], whole, 0, t)
 
         y = {}
 
-        def second_pass(h, a, codes, scales, m0):
-            for i in range(4):
-                if a == 0:
-                    y[h, i] = bank(4 * h + i, "second")
-                for n in range(2):
-                    col = H * a + P * (2 * i + n)
-                    for c in range(HALF // CHUNK):
-                        nc.tensor.matmul_mx(
-                            out=y[h, i][:, HALF * n + CHUNK * c : HALF * n + CHUNK * (c + 1)],
-                            lhsT=w2w[:, 2 * col : 2 * (col + P)].bitcast(FP4X4),
-                            lhsT_scale=w2s[:, col : col + P],
-                            rhs=codes[:, m0 + CHUNK * c : m0 + CHUNK * (c + 1)].bitcast(FP8X4),
-                            rhs_scale=scales[:, m0 + CHUNK * c : m0 + CHUNK * (c + 1)],
-                            start=(a == 0 and n == 0 and c == 0),
-                            stop=(a == BLOCKS - 1 and n == 1 and c == HALF // CHUNK - 1),
-                        )
+        def second_pass(h, i, a, x, m0):
+            if a == 0:
+                y[h, i] = bank(4 * h + i, "second")
+            for n in range(2):
+                col = H * a + P * (2 * i + n)
+                for c in range(HALF // CHUNK):
+                    nc.tensor.matmul_mx(
+                        out=y[h, i][:, HALF * n + CHUNK * c : HALF * n + CHUNK * (c + 1)],
+                        lhsT=w2w[:, 2 * col : 2 * (col + P)].bitcast(FP4X4),
+                        lhsT_scale=w2s[:, col : col + P],
+                        rhs=x[0][:, m0 + CHUNK * c : m0 + CHUNK * (c + 1)].bitcast(FP8X4),
+                        rhs_scale=x[1][:, m0 + CHUNK * c : m0 + CHUNK * (c + 1)],
+                        start=(a == 0 and n == 0 and c == 0),
+                        stop=(a == BLOCKS - 1 and n == 1 and c == HALF // CHUNK - 1),
+                    )
 
-        for t in range(PACK + 1):
-            if t < PACK:
-                pick_early(ring[t % 2], 1, t, 0, HALF)
-            if t > 0:
-                times_late(prod1[0][:, t - 1, :], ring[(t - 1) % 2], 1, t - 1, 0, HALF)
-        for t in range(PACK):
-            sine_rows(rows1[0][:], prod1[0][:, t, :], 1, t, HALF)
-        weave(nc.scalar.copy, woven1[0][:].bitcast(BF16), rows1[0][:])
+        def rows1_flat(h):
+            return rows1[:, h].rearrange("p t m -> p (t m)")
 
-        early1 = [ring[0], ring[1], rows0[:, 0:HALF], woven0[:, 0:HALF]]
-        last = [prod1[1][:, 0, :], prod1[1][:, 1, :], prod1[1][:, 2, :], woven1[0][:, 0:HALF]]
-        pick_early(early1[0], 1, 0, HALF, M)
-        pick_early(early1[1], 1, 1, HALF, M)
-        times_late(last[0], early1[0], 1, 0, HALF, M)
+        for t in range(2):
+            picks(1, t, range(2))
+            products(1, t, range(2))
+            sine_rows(rows1[:, :, t, :], prod_buf[:, 3 + t, :], 1, t)
+        picks(1, 2, range(2))
+        products(1, 2, [0])
+        sine_rows(rows1[:, 0, 2, :], prod[1, 2, 0], 1, 2)
+        picks(1, 3, [0])
         weave(nc.vector.tensor_copy, woven0[:].bitcast(BF16), rows0[:].bitcast(BF16))
-        pick_early(early1[2], 1, 2, HALF, M)
-        times_late(last[1], early1[1], 1, 1, HALF, M)
+        products(1, 3, [0])
+        sine_rows(rows1[:, 0, 3, :], prod[1, 3, 0], 1, 3)
+        weave(nc.scalar.copy, woven1[0][:].bitcast(BF16), rows1_flat(0))
         x0 = quantize_x("x0", woven0[:].bitcast(BF16), M)
-        pick_early(early1[3], 1, 3, HALF, M)
-        times_late(last[2], early1[2], 1, 2, HALF, M)
+        picks(1, 3, [1])
+        products(1, 2, [1])
+        sine_rows(rows1[:, 1, 2, :], prod[1, 2, 1], 1, 2)
         x10 = quantize_x("x10", woven1[0][:].bitcast(BF16), HALF)
-        times_late(last[3], early1[3], 1, 3, HALF, M)
-        nc.gpsimd.tensor_copy(probe[:, 1:2], last[3][:, 0:1])
-        second_pass(0, 0, x0[0], x0[1], 0)
-        second_pass(0, 1, x10[0], x10[1], 0)
-        second_pass(1, 0, x0[0], x0[1], HALF)
-        for t in range(PACK):
-            sine_rows(rows1[1][:], last[t], 1, t, HALF)
-        weave(nc.scalar.copy, woven1[1][:].bitcast(BF16), rows1[1][:])
+        products(1, 3, [1])
+        nc.gpsimd.tensor_copy(probe[:, 1:2], prod[1, 3, 1][:, 0:1])
+        sine_rows(rows1[:, 1, 3, :], prod[1, 3, 1], 1, 3)
+        weave(nc.scalar.copy, woven1[1][:].bitcast(BF16), rows1_flat(1))
+        for i in range(4):
+            second_pass(0, i, 0, x0, 0)
+            second_pass(0, i, 1, x10, 0)
+        for i in range(4):
+            second_pass(1, i, 0, x0, HALF)
 
         out_rows = out.rearrange("(b p t) m -> b p t m", b=BLOCKS, t=PACK)
 
         def finish(h, banks):
             for i in banks:
                 b = i // 2
+                t0 = 2 * (i % 2)
                 if (h, i) == (0, 3):
                     res = woven1[1][:].rearrange("p (n m) -> p n m", n=2)
                 else:
                     res = sb("res%d_%d" % (h, i), [P, 2, HALF], F32)
                 for n in range(2):
-                    t = 2 * (i % 2) + n
-                    if b == 0:
-                        src = prod[0, t][:, HALF * h : HALF * (h + 1)]
-                    elif h == 0:
-                        src = prod1[0][:, t, :]
-                    else:
-                        src = last[t]
+                    t = t0 + n
                     nc.vector.scalar_tensor_tensor(
-                        res[:, n, :], src, gain2[:, b, t : t + 1], y[h, i][:, HALF * n : HALF * (n + 1)], MULT, ADD
+                        res[:, n, :], prod[b, t, h], gain2[:, b, t : t + 1], half(y[h, i], n), MULT, ADD
                     )
-                t0 = 2 * (i % 2)
                 nc.sync.dma_start(out_rows[b][:, t0 : t0 + 2, HALF * h : HALF * (h + 1)], res[:])
 
         finish(0, range(3))
         x11 = quantize_x("x11", woven1[1][:].bitcast(BF16), HALF)
-        second_pass(1, 1, x11[0], x11[1], 0)
+        for i in range(4):
+            second_pass(1, i, 1, x11, 0)
         finish(0, range(3, 4))
         finish(1, range(4))

from contextlib import ExitStack

import concourse.mybir as mybir

K, H, T, S, M = 1536, 1024, 2048, 1024, 512
FLOPS = 2 * K * H * S + 2 * H * H * M

F32 = mybir.dt.float32
BF16 = mybir.dt.bfloat16
I32 = mybir.dt.int32
U32 = mybir.dt.uint32
U16 = mybir.dt.uint16
U8 = mybir.dt.uint8
FP8X4 = mybir.dt.float8_e4m3fn_x4
FP4X4 = mybir.dt.float4_e2m1fn_x4
ACT = mybir.ActivationFunctionType
MULT = mybir.AluOpType.mult
ADD = mybir.AluOpType.add

P = 128
PACK = 4
PASS = P * PACK
BANK = 512
K_PASSES = K // PASS
BLOCKS = H // PASS
HALF = M // 2
CHUNK = 128
PLANE_ROW = (0, 8, 4)
HEAD_SHARE = 84
TURN_SHARE = 40


def tile_list_hatchery_turning_outlooks_kernel(
    tc, tab_words, tab_scales, offs, pos1, pos2, w1, gain, carry, w2_words, w2_scales, out
):
    nc = tc.nc
    with ExitStack() as ctx:
        keep = ctx.enter_context(tc.tile_pool(name="keep", bufs=1))
        psum = ctx.enter_context(tc.psum_pool(name="psum", bufs=1))

        def sb(name, shape, dtype, after=None):
            return keep.tile(shape, dtype, name=name, tag=after or name, align_bytes=64)

        def bank(i, stage):
            return psum.tile([P, BANK], F32, name="%s_bank%d" % (stage, i), tag="bank%d" % i)

        offs_t = keep.tile([P, S // 16], U16, name="offs_t")
        pos1_t = keep.tile([P, M // 16], U16, name="pos1_t")
        pos2_t = keep.tile([P, M // 16], U16, name="pos2_t")

        scale_window = sb("scale_window", [P, T], U8)
        scale_picked = sb("scale_picked", [P, S], U8)
        v_scales = sb("v_scales", [P, S], U8)
        w2s_raw = sb("w2s_raw", [P, BLOCKS, H], U8)
        warm = sb("warm", [P, 2], F32)

        nc.gpsimd.memset(scale_window[:].bitcast(I32), 0)
        nc.gpsimd.memset(warm[:, 0:1], 0.0)
        nc.vector.memset(v_scales[:].bitcast(I32), 0)
        nc.vector.memset(w2s_raw[:].rearrange("p a c -> p (a c)").bitcast(I32), 0)

        tab = [sb("tab%d" % a, [P, T], I32) for a in range(K_PASSES)]

        def load_tab(a):
            nc.sync.dma_start(tab[a][:], tab_words[a].rearrange("p t i -> p (t i)").bitcast(I32))

        nc.sync.dma_start(offs_t[:], offs)
        load_tab(0)
        rows = tab_scales.rearrange("a (g e) t -> e g a t", e=2)
        for e in range(2):
            nc.sync.dma_start(scale_window[e:P:8, :].bitcast(I32), rows[e][:, 0:2, :].bitcast(I32))
        for e in range(2):
            nc.sync.dma_start(scale_window[4 + e : P : 16, :].bitcast(I32), rows[e][:, 2, :].bitcast(I32))
        nc.scalar.activation(warm[:, 1:2], warm[:, 0:1], ACT.Silu)


        raw = {}

        def load_w1(b, a, after=None):
            raw[b, a] = sb("raw%d_%d" % (b, a), [P, PACK, PASS], F32, after)
            src = w1[PASS * a : PASS * (a + 1), PASS * b : PASS * (b + 1)]
            nc.sync.dma_start(raw[b, a][:], src.rearrange("(p j) c -> p j c", j=PACK))

        nc.sync.dma_start(pos1_t[:], pos1)
        nc.sync.dma_start(pos2_t[:], pos2)
        for d in range(4):
            nc.gpsimd.dma_start(
                w2s_raw[32 * d : 32 * d + 4, :, :].bitcast(I32),
                w2_scales[:, 4 * d : 4 * d + 4, :].rearrange("a r c -> r a c").bitcast(I32),
            )
        load_w1(0, 0)
        load_tab(1)
        load_tab(2)
        load_w1(0, 1)

        v_words = [sb("v_words%d" % a, [P, S], U32) for a in range(K_PASSES)]

        def gather_tab(a):
            nc.vector.tensor_copy(v_words[a][:], tab[a][:].bitcast(U32).indirect(offs_t[:]))

        grouped = {}
        w1_codes = {}
        w1_scales = {}
        for b in range(BLOCKS):
            for a in range(K_PASSES):
                grouped[b, a] = sb("grouped%d_%d" % (b, a), [P, PASS * PACK // 2], F32)
                w1_codes[b, a] = sb("w1_codes%d_%d" % (b, a), [P, PASS], U32)
                w1_scales[b, a] = sb("w1_scales%d_%d" % (b, a), [P, PASS], U8)

        def deal_w1(copy, b, a, q0, q1):
            dst = grouped[b, a][:].bitcast(BF16).rearrange("p (u v q j) -> p u q j v", u=2, v=2, j=PACK)
            src = raw[b, a][:].rearrange("p j (q u v) -> p u q j v", u=2, v=2)
            copy(dst[:, :, q0:q1], src[:, :, q0:q1])

        def quantize_w1(b, a, t0, t1):
            nc.vector.quantize_mx(
                out=w1_codes[b, a][:, P * t0 : P * t1].bitcast(FP8X4),
                scales=w1_scales[b, a][:, P * t0 : P * t1],
                in_=grouped[b, a][:].bitcast(BF16)[:, PASS * t0 : PASS * t1],
            )

        acc = {}

        def first_pass(b, a, t):
            for c in range(S // BANK):
                if a == 0:
                    acc[b, t, c] = bank(4 * b + 2 * (t % 2) + c, "first%d_%d" % (b, t))
                nc.tensor.matmul_mx(
                    out=acc[b, t, c][:],
                    lhsT=w1_codes[b, a][:, P * t : P * (t + 1)].bitcast(FP8X4),
                    lhsT_scale=w1_scales[b, a][:, P * t : P * (t + 1)],
                    rhs=v_words[a][:, BANK * c : BANK * (c + 1)].bitcast(FP8X4),
                    rhs_scale=v_scales[PLANE_ROW[a] : P, BANK * c : BANK * (c + 1)],
                    start=(a == 0),
                    stop=(a == K_PASSES - 1),
                )

        def first_product(b, t):
            for a in range(K_PASSES):
                first_pass(b, a, t)

        th = {}

        def tanh_rows(b, t):
            th[b, t] = sb("th%d_%d" % (b, t), [P, S], F32)
            for c in range(S // BANK):
                nc.scalar.activation(th[b, t][:, BANK * c : BANK * (c + 1)], acc[b, t, c][:], ACT.Tanh)

        gather_tab(0)
        nc.vector.tensor_copy(scale_picked[:], scale_window[:].indirect(offs_t[:]))
        for e in range(2):
            nc.sync.dma_start(v_scales[e:P:4, :].bitcast(I32), scale_picked[e:P:4, :].bitcast(I32))
        for e in range(2):
            nc.sync.dma_start(
                v_scales[2 + e : 2 + e + P - 16 : 4, :].bitcast(I32), scale_picked[16 + e : P : 4, :].bitcast(I32)
            )
        load_w1(0, 2, after="scale_window")
        deal_w1(nc.scalar.copy, 0, 0, 0, P)
        gather_tab(1)
        w2w_raw = sb("w2w_raw", [P, BLOCKS, 2 * H], U8, after="tab1")
        nc.sync.dma_start(w2w_raw[:].bitcast(I32), w2_words.rearrange("a p c -> p a c").bitcast(I32))
        quantize_w1(0, 0, 0, PACK)
        gather_tab(2)
        load_w1(1, 0, after="grouped0_0")
        gain_t = sb("gain_t", [P, BLOCKS, PACK], F32, after="scale_picked")
        carry_t = sb("carry_t", [P, BLOCKS, PACK], F32, after="raw0_0")
        gain2 = sb("gain2", [P, BLOCKS, PACK], F32)
        nc.sync.dma_start(gain_t[:], gain.rearrange("(b p t) -> p b t", b=BLOCKS, t=PACK))
        nc.sync.dma_start(carry_t[:], carry.rearrange("(b p t) -> p b t", b=BLOCKS, t=PACK))
        deal_w1(nc.scalar.copy, 0, 1, 0, P)
        load_w1(1, 1, after="raw0_1")
        deal_w1(nc.vector.tensor_copy, 0, 2, 0, HEAD_SHARE)
        deal_w1(nc.scalar.copy, 0, 2, HEAD_SHARE, P)
        load_w1(1, 2, after="scale_window")
        for t0, t1 in ((0, 1), (1, 2), (2, 4)):
            quantize_w1(0, 1, t0, t1)
            quantize_w1(0, 2, t0, t1)
            if t0 < 2:
                first_product(0, t0)
        nc.scalar.activation(gain2[:], gain_t[:], ACT.Square)

        w2w = sb("w2w", [P, BLOCKS * 2 * H], U8)
        w2s = sb("w2s", [P, BLOCKS * H], U8, after="tab2")
        nc.vector.tensor_copy(
            w2w[:].bitcast(U16).rearrange("p (k t c i) -> p k c t i", t=PACK, c=16, i=8),
            w2w_raw[:].rearrange("p a c -> p (a c)").bitcast(U16).rearrange("p (k c i t) -> p k c t i", t=PACK, c=16, i=8),
        )
        nc.vector.tensor_copy(
            w2s[:].rearrange("p (k t c i) -> p k c t i", t=PACK, c=8, i=16),
            w2s_raw[:].rearrange("p a c -> p (a c)").rearrange("p (k c i t) -> p k c t i", t=PACK, c=8, i=16),
        )

        def half(ap, h):
            return ap[:, HALF * h : HALF * (h + 1)]

        def pick_early(dst, b, t, h):
            nc.vector.tensor_copy(dst, th[b, t][:].indirect(pos1_t[:, 16 * h : 16 * (h + 1)]))

        def times_late(dst, early_half, b, t, h):
            nc.vector.tensor_tensor(dst, th[b, t][:].indirect(pos2_t[:, 16 * h : 16 * (h + 1)]), early_half, MULT)

        early_buf = sb("early_buf", [P, 2, M], F32)
        prod_buf = sb("prod_buf", [P, 6, M], F32)
        rows0 = sb("rows0", [P, PACK * M // 2], F32)
        woven0 = sb("woven0", [P, PACK * M // 2], F32)
        rows1 = sb("rows1", [P, 2, PACK, HALF], BF16)
        woven1 = [sb("woven1_%d" % h, [P, PACK * HALF // 2], F32) for h in range(2)]

        early = {}
        prod = {}
        for h in range(2):
            for t in range(2):
                early[0, t, h] = half(early_buf[:, t, :], h)
                early[0, t + 2, h] = half(grouped[1, t][:, 0:M], h)
                early[1, t, h] = half(early_buf[:, t, :], h)
                early[1, t + 2, h] = half(early_buf[:, t, :], h)
                prod[1, t, h] = half(prod_buf[:, 3 + t, :], h)
            for t in range(3):
                prod[0, t, h] = half(prod_buf[:, t, :], h)
            prod[0, 3, h] = half(grouped[1, 2][:, 0:M], h)
        early[1, 3, 1] = woven0[:, 0:HALF]
        prod[1, 2, 0] = prod_buf[:, 5, 0:HALF]
        prod[1, 3, 0] = rows0[:, 0:HALF]
        prod[1, 2, 1] = woven0[:, HALF:M]
        prod[1, 3, 1] = woven1[0][:, 0:HALF]

        def picks(b, t, halves):
            for h in halves:
                pick_early(early[b, t, h], b, t, h)

        def products(b, t, halves):
            for h in halves:
                times_late(prod[b, t, h], early[b, t, h], b, t, h)

        tanh_rows(0, 0)
        probe = sb("probe", [P, 2], F32)
        nc.gpsimd.tensor_copy(probe[:, 0:1], th[0, 0][:, S - 1 : S])
        first_product(0, 2)
        tanh_rows(0, 1)
        first_product(0, 3)
        deal_w1(nc.scalar.copy, 1, 0, 0, P)
        tanh_rows(0, 2)
        deal_w1(nc.scalar.copy, 1, 1, 0, P)
        tanh_rows(0, 3)
        deal_w1(nc.vector.tensor_copy, 1, 2, 0, TURN_SHARE)
        deal_w1(nc.scalar.copy, 1, 2, TURN_SHARE, P)
        for t in range(PACK):
            if t >= 2:
                quantize_w1(1, t - 2, 0, PACK)
            picks(0, t, range(2))
            if t == PACK - 1:
                quantize_w1(1, 2, 0, 2)
                quantize_w1(1, 2, 2, PACK)
            products(0, t, range(2))
        for t in range(PACK):
            first_product(1, t)
            tanh_rows(1, t)

        sines = raw[1, 2]

        def sine_rows(dst, src, b, t):
            width = src.shape[1]
            s = sines[:, t % 2, 0:width]
            nc.scalar.activation(s, src, ACT.Sin, scale=gain2[:, b, t : t + 1])
            if width == M:
                s = s.rearrange("p (h m) -> p h m", h=2)
            nc.scalar.activation(dst, s, ACT.Copy, scale=carry_t[:, b, t : t + 1])

        def weave(copy, woven_bf, rows_bf):
            copy(
                woven_bf.rearrange("p (c i t) -> p c t i", i=4, t=PACK),
                rows_bf.rearrange("p (t c i) -> p c t i", i=4, t=PACK),
            )

        def quantize_x(name, woven_bf, width):
            codes = sb(name + "_codes", [P, width], U32)
            scales = sb(name + "_scales", [P, width], U8)
            nc.vector.quantize_mx(out=codes[:].bitcast(FP8X4), scales=scales[:], in_=woven_bf)
            return codes, scales

        rows0_bf = rows0[:].bitcast(BF16).rearrange("p (t h m) -> p t h m", t=PACK, h=2)
        for t in range(PACK):
            whole = prod_buf[:, t, :] if t < 3 else grouped[1, 2][:, 0:M]
            sine_rows(rows0_bf[:, t], whole, 0, t)

        y = {}

        def second_pass(h, i, a, x, m0):
            if a == 0:
                y[h, i] = bank(4 * h + i, "second")
            for n in range(2):
                col = H * a + P * (2 * i + n)
                for c in range(HALF // CHUNK):
                    nc.tensor.matmul_mx(
                        out=y[h, i][:, HALF * n + CHUNK * c : HALF * n + CHUNK * (c + 1)],
                        lhsT=w2w[:, 2 * col : 2 * (col + P)].bitcast(FP4X4),
                        lhsT_scale=w2s[:, col : col + P],
                        rhs=x[0][:, m0 + CHUNK * c : m0 + CHUNK * (c + 1)].bitcast(FP8X4),
                        rhs_scale=x[1][:, m0 + CHUNK * c : m0 + CHUNK * (c + 1)],
                        start=(a == 0 and n == 0 and c == 0),
                        stop=(a == BLOCKS - 1 and n == 1 and c == HALF // CHUNK - 1),
                    )

        def rows1_flat(h):
            return rows1[:, h].rearrange("p t m -> p (t m)")

        for t in range(2):
            picks(1, t, range(2))
            products(1, t, range(2))
            sine_rows(rows1[:, :, t, :], prod_buf[:, 3 + t, :], 1, t)
        picks(1, 2, range(2))
        products(1, 2, [0])
        sine_rows(rows1[:, 0, 2, :], prod[1, 2, 0], 1, 2)
        picks(1, 3, [0])
        weave(nc.vector.tensor_copy, woven0[:].bitcast(BF16), rows0[:].bitcast(BF16))
        products(1, 3, [0])
        sine_rows(rows1[:, 0, 3, :], prod[1, 3, 0], 1, 3)
        weave(nc.scalar.copy, woven1[0][:].bitcast(BF16), rows1_flat(0))
        x0 = quantize_x("x0", woven0[:].bitcast(BF16), M)
        picks(1, 3, [1])
        products(1, 2, [1])
        sine_rows(rows1[:, 1, 2, :], prod[1, 2, 1], 1, 2)
        x10 = quantize_x("x10", woven1[0][:].bitcast(BF16), HALF)
        products(1, 3, [1])
        nc.gpsimd.tensor_copy(probe[:, 1:2], prod[1, 3, 1][:, 0:1])
        sine_rows(rows1[:, 1, 3, :], prod[1, 3, 1], 1, 3)
        weave(nc.scalar.copy, woven1[1][:].bitcast(BF16), rows1_flat(1))
        for i in range(4):
            second_pass(0, i, 0, x0, 0)
            second_pass(0, i, 1, x10, 0)
        for i in range(4):
            second_pass(1, i, 0, x0, HALF)

        out_rows = out.rearrange("(b p t) m -> b p t m", b=BLOCKS, t=PACK)

        def finish(h, banks):
            for i in banks:
                b = i // 2
                t0 = 2 * (i % 2)
                if (h, i) == (0, 3):
                    res = woven1[1][:].rearrange("p (n m) -> p n m", n=2)
                else:
                    res = sb("res%d_%d" % (h, i), [P, 2, HALF], F32)
                for n in range(2):
                    t = t0 + n
                    nc.vector.scalar_tensor_tensor(
                        res[:, n, :], prod[b, t, h], gain2[:, b, t : t + 1], half(y[h, i], n), MULT, ADD
                    )
                nc.sync.dma_start(out_rows[b][:, t0 : t0 + 2, HALF * h : HALF * (h + 1)], res[:])

        finish(0, range(3))
        x11 = quantize_x("x11", woven1[1][:].bitcast(BF16), HALF)
        for i in range(4):
            second_pass(1, i, 1, x11, 0)
        finish(0, range(3, 4))
        finish(1, range(4))
